import numpy as np, ml_dtypes
CORES = [24,26,29,31,48,50,53,55]
N = 8
C = 512
def setup_inputs(rng):
    x = 150 * rng.standard_normal((1, 128, C), dtype=np.float32) + 2 * rng.standard_normal((N, 128, C), dtype=np.float32)
    x = (x + rng.uniform(100, 300, (1, 128, C)) * (rng.random((1, 128, C)) < 0.7) * (rng.random((N, 128, C)) < 0.5)).astype(np.float32)
    return {"x": x}
def setup_inputs_trail(rng):
    d = setup_inputs(rng); x = d["x"].copy(); t = int(rng.integers(N))
    x[t] = np.delete(x, t, axis=0).max(axis=0) - rng.uniform(3.0, 20.0, x[t].shape).astype(np.float32)
    return {"x": x}
def reference(x):
    X = x.astype(np.float64)
    P = np.exp(X - X.max(axis=0))
    return {"y": (P / P.sum(axis=0)).astype(ml_dtypes.bfloat16)}

@@ -1,0 +1,213 @@
+from concourse.bass import DstId, RemoteDMATransfer
+from concourse.mybir import AluOpType, ActivationFunctionType
+
+W = 128
+NPOOL = 40
+SCRATCH = {
+    "xs": ("sbuf", [128, 512], "float32"),
+    "land": ("sbuf", [128, 512], "float32"),
+    "t1": ("sbuf", [128, W], "float32"),
+    "t2": ("sbuf", [128, W], "float32"),
+    "mt": ("sbuf", [128, W], "bfloat16"),
+    "mrem": ("sbuf", [128, W], "bfloat16"),
+    "ssb": ("sbuf", [128, W], "bfloat16"),
+    "srem": ("sbuf", [128, W], "bfloat16"),
+    "d": ("sbuf", [128, 512], "float32"),
+    "p": ("sbuf", [128, 512], "bfloat16"),
+    "ones": ("sbuf", [128, 128], "bfloat16"),
+    "ident": ("sbuf", [128, 128], "bfloat16"),
+    "dd": ("sbuf", [128, W], "float32"),
+    "den": ("sbuf", [128, W], "float32"),
+    "ys": ("sbuf", [128, 512], "bfloat16"),
+    "yb": ("sbuf", [128, 512], "bfloat16"),
+    "ps_s": ("psum", [128, 512], "float32"),
+    "ps_e": ("psum", [128, 512], "float32"),
+    "ps_t": ("psum", [128, 512], "float32"),
+    "ps_w": ("psum", [128, 512], "float32"),
+}
+SEMAPHORES = ["loaded", "stored", "xarr", "marr", "sarr", "yarr", "sent"] + ["c%d" % i for i in range(NPOOL)]
+
+
+def _bits(m):
+    return [i for i in range(m.bit_length()) if (m >> i) & 1]
+
+
+def _mask_of(engines):
+    m = 0
+    for e in engines:
+        m |= 1 << e
+    return m
+
+
+def _deal(topo, core, dsts):
+    eng = _bits(topo.mask(core, dsts[0]))
+    per = 1
+    while per * 2 * len(dsts) <= len(eng):
+        per *= 2
+    pool = eng[0::2] + eng[1::2]
+    order = [c for c in dsts if topo.die(c) != topo.die(core)] + [c for c in dsts if topo.die(c) == topo.die(core)]
+    return {c: pool[i * per:(i + 1) * per] for i, c in enumerate(order)}
+
+
+def rank_program(g, core, T, topo):
+    chips = sorted(set(topo.chip(c) for c in T.cores))
+    here = topo.chip(core)
+    if here not in chips:
+        return
+    ranks_of = {ch: [c for c in T.cores if topo.chip(c) == ch] for ch in chips}
+    there = [ch for ch in chips if ch != here][0]
+
+    def reducers(ch, other):
+        far = ranks_of[other][0]
+        cs = [c for c in range(topo.CORES_PER_CHIP * topo.CHIPS) if topo.chip(c) == ch and topo.may_write(c, far)]
+        return sorted(cs, key=lambda c: (topo.die(c), c))
+
+    red = reducers(here, there)
+    red_far = reducers(there, here)
+    local = ranks_of[here]
+    is_rank = core in local
+    is_red = core in red
+    if not (is_rank or is_red):
+        return
+
+    V, S, PE, Q = g.vector, g.scalar, g.tensor, g.sync
+    sem = T.sem
+    used = [0]
+
+    def new_sem():
+        s = sem["c%d" % used[0]]
+        used[0] += 1
+        return s
+
+    def vtt(out, a, b, op):
+        s = new_sem()
+        V.tensor_tensor(out, a, b, op).then_inc(s, 1)
+        return s
+
+    sent = 0
+    if is_red:
+        s_ones, s_id = new_sem(), new_sem()
+        V.memset(T.ones[:], 1.0).then_inc(s_ones, 1)
+        g.wait_ge(s_ones, 1)
+        g.affine_select(T.ident[:], T.ones[:], [[-1, 128]], AluOpType.is_equal, 0.0, 0, 1).then_inc(s_id, 1)
+
+    if is_rank:
+        j_me = local.index(core)
+        Q.dma_start(T.xs[:], T.x[:]).then_inc(sem.loaded, 16)
+        g.wait_ge(sem.loaded, 16)
+        dsts = [c for c in red if c != core]
+        eng = _deal(topo, core, dsts)
+        trs = []
+        for c in dsts:
+            k = red.index(c)
+            rid, pid, _ = topo.addr(c)
+            trs.append(RemoteDMATransfer(dst_ids=[DstId(rid=rid, pnc=pid)], dma_engine_mask=_mask_of(eng[c]),
+                                         remote_sem=sem.xarr, src=T.xs[:, k * W:(k + 1) * W],
+                                         dst=T.land[:, j_me * W:(j_me + 1) * W]))
+            sent += len(eng[c])
+        g.remote_dma_fused(trs, local_sem=sem.sent)
+
+    own_y = None
+    if is_red:
+        k_me = red.index(core)
+        partner = red_far[k_me]
+        prid, ppid, _ = topo.addr(partner)
+        pmask = topo.mask(core, partner)
+        npe = len(_bits(pmask))
+
+        def blk(j, a, b):
+            if local[j] == core:
+                return T.xs[:, k_me * W + a:k_me * W + b]
+            return T.land[:, j * W + a:j * W + b]
+
+        n_x = sum(len(_deal(topo, c, [r for r in red if r != c])[core]) for c in local if c != core)
+        V.wait_ge(sem.xarr, n_x)
+        if is_rank:
+            V.wait_ge(sem.loaded, 16)
+
+        def shift(a, b):
+            s1 = vtt(T.t1[:, a:b], blk(0, a, b), blk(1, a, b), AluOpType.max)
+            s2 = vtt(T.t2[:, a:b], blk(2, a, b), blk(3, a, b), AluOpType.max)
+            V.wait_ge(s1, 1)
+            V.wait_ge(s2, 1)
+            s3 = vtt(T.mt[:, a:b], T.t1[:, a:b], T.t2[:, a:b], AluOpType.max)
+            V.wait_ge(s3, 1)
+            return s3
+
+        def weights(j, a, b):
+            sd = vtt(T.d[:, j * W + a:j * W + b], blk(j, a, b), T.mt[:, a:b], AluOpType.subtract)
+            S.wait_ge(sd, 1)
+            sp = new_sem()
+            S.activation(T.p[:, j * W + a:j * W + b], T.d[:, j * W + a:j * W + b],
+                         ActivationFunctionType.Exp).then_inc(sp, 1)
+            return sp
+
+        H = 32
+        s_ma = shift(0, H)
+        sp = {0: [weights(0, 0, H)]}
+        s_mb = shift(H, W)
+        g.wait_ge(s_ma, 1)
+        g.wait_ge(s_mb, 1)
+        g.remote_dma(T.mrem[:], T.mt[:], sem.marr, sem.sent, ppid, prid, pmask)
+        sent += npe
+        sp[0].append(weights(0, H, W))
+        for j in range(1, len(local)):
+            sp[j] = [weights(j, 0, W)]
+        PE.wait_ge(s_id, 1)
+        s_sum = new_sem()
+        for j in range(len(local)):
+            for s in sp[j]:
+                PE.wait_ge(s, 1)
+            mm = PE.matmul(T.ps_s[:, 0:W], T.ident[:], T.p[:, j * W:(j + 1) * W], j == 0, j == len(local) - 1)
+        mm.then_inc(s_sum, 1)
+        V.wait_ge(s_sum, 1)
+        s_cp = new_sem()
+        V.tensor_copy(T.ssb[:], T.ps_s[:, 0:W]).then_inc(s_cp, 1)
+        g.wait_ge(s_cp, 1)
+        g.remote_dma(T.srem[:], T.ssb[:], sem.sarr, sem.sent, ppid, prid, pmask)
+        sent += npe
+
+        V.wait_ge(sem.marr, npe)
+        s_dd = vtt(T.dd[:], T.mrem[:], T.mt[:], AluOpType.subtract)
+        V.wait_ge(s_dd, 1)
+        s_cl = new_sem()
+        V.tensor_scalar(T.dd[:], T.dd[:], 60.0, None, AluOpType.min).then_inc(s_cl, 1)
+        S.wait_ge(s_cl, 1)
+        s_e = new_sem()
+        S.activation(T.ps_e[:, 0:W], T.dd[:], ActivationFunctionType.Exp).then_inc(s_e, 1)
+        V.wait_ge(s_cp, 1)
+        V.wait_ge(s_e, 1)
+        V.wait_ge(sem.sarr, npe)
+        s_t = vtt(T.ps_t[:, 0:W], T.srem[:], T.ps_e[:, 0:W], AluOpType.mult)
+        V.wait_ge(s_t, 1)
+        s_den = vtt(T.den[:], T.ps_t[:, 0:W], T.ssb[:], AluOpType.add)
+        V.wait_ge(s_den, 1)
+        s_w = new_sem()
+        V.reciprocal(T.ps_w[:, 0:W], T.den[:]).then_inc(s_w, 1)
+        V.wait_ge(s_w, 1)
+
+        dsts = [c for c in local if c != core]
+        eng = _deal(topo, core, dsts)
+        trs = []
+        for c in dsts:
+            j = local.index(c)
+            s_y = vtt(T.ys[:, j * W:(j + 1) * W], T.p[:, j * W:(j + 1) * W], T.ps_w[:, 0:W], AluOpType.mult)
+            g.wait_ge(s_y, 1)
+            rid, pid, _ = topo.addr(c)
+            trs.append(RemoteDMATransfer(dst_ids=[DstId(rid=rid, pnc=pid)], dma_engine_mask=_mask_of(eng[c]),
+                                         remote_sem=sem.yarr, src=T.ys[:, j * W:(j + 1) * W],
+                                         dst=T.yb[:, k_me * W:(k_me + 1) * W]))
+            sent += len(eng[c])
+        g.remote_dma_fused(trs, local_sem=sem.sent)
+        if is_rank:
+            own_y = vtt(T.yb[:, k_me * W:(k_me + 1) * W], T.p[:, j_me * W:(j_me + 1) * W], T.ps_w[:, 0:W],
+                        AluOpType.mult)
+
+    if is_rank:
+        n_y = sum(len(_deal(topo, r, [c for c in local if c != r])[core]) for r in red if r != core)
+        Q.wait_ge(sem.yarr, n_y)
+        if own_y is not None:
+            Q.wait_ge(own_y, 1)
+        Q.dma_start(T.y[:], T.yb[:]).then_inc(sem.stored, 16)
+        Q.wait_ge(sem.stored, 16)
+    g.wait_ge(sem.sent, sent)

@@ -2,7 +2,7 @@ from concourse.bass import DstId, RemoteDMATransfer
 from concourse.mybir import AluOpType, ActivationFunctionType
 
 W = 128
-NPOOL = 40
+NPOOL = 48
 SCRATCH = {
     "xs": ("sbuf", [128, 512], "float32"),
     "land": ("sbuf", [128, 512], "float32"),
@@ -14,15 +14,20 @@ SCRATCH = {
     "srem": ("sbuf", [128, W], "bfloat16"),
     "d": ("sbuf", [128, 512], "float32"),
     "p": ("sbuf", [128, 512], "bfloat16"),
-    "ones": ("sbuf", [128, 128], "bfloat16"),
+    "zer": ("sbuf", [128, 128], "float32"),
+    "sel": ("sbuf", [128, 128], "float32"),
     "ident": ("sbuf", [128, 128], "bfloat16"),
     "dd": ("sbuf", [128, W], "float32"),
     "den": ("sbuf", [128, W], "float32"),
     "ys": ("sbuf", [128, 512], "bfloat16"),
     "yb": ("sbuf", [128, 512], "bfloat16"),
-    "ps_s": ("psum", [128, 512], "float32"),
+    "xp0": ("psum", [128, 512], "float32"),
+    "xp1": ("psum", [128, 512], "float32"),
+    "xp2": ("psum", [128, 512], "float32"),
+    "xp3": ("psum", [128, 512], "float32"),
+    "ps_a": ("psum", [128, 512], "float32"),
+    "ps_b": ("psum", [128, 512], "float32"),
     "ps_e": ("psum", [128, 512], "float32"),
-    "ps_t": ("psum", [128, 512], "float32"),
     "ps_w": ("psum", [128, 512], "float32"),
 }
 SEMAPHORES = ["loaded", "stored", "xarr", "marr", "sarr", "yarr", "sent"] + ["c%d" % i for i in range(NPOOL)]
@@ -70,7 +75,14 @@ def rank_program(g, core, T, topo):
     if not (is_rank or is_red):
         return
 
+    def send_deal(c):
+        return _deal(topo, c, [r for r in red if r != c])
+
+    def ret_deal(r):
+        return _deal(topo, r, [c for c in local if c != r])
+
     V, S, PE, Q = g.vector, g.scalar, g.tensor, g.sync
+    Exp, Copy = ActivationFunctionType.Exp, ActivationFunctionType.Copy
     sem = T.sem
     used = [0]
 
@@ -84,21 +96,28 @@ def rank_program(g, core, T, topo):
         V.tensor_tensor(out, a, b, op).then_inc(s, 1)
         return s
 
+    def act(out, in_, func):
+        s = new_sem()
+        S.activation(out, in_, func).then_inc(s, 1)
+        return s
+
     sent = 0
     if is_red:
-        s_ones, s_id = new_sem(), new_sem()
-        V.memset(T.ones[:], 1.0).then_inc(s_ones, 1)
-        g.wait_ge(s_ones, 1)
-        g.affine_select(T.ident[:], T.ones[:], [[-1, 128]], AluOpType.is_equal, 0.0, 0, 1).then_inc(s_id, 1)
+        s_zer, s_sel = new_sem(), new_sem()
+        V.memset(T.zer[:], 0.0).then_inc(s_zer, 1)
+        g.wait_ge(s_zer, 1)
+        g.affine_select(T.sel[:], T.zer[:], [[-1, 128]], AluOpType.is_equal, -200.0, 0, 1).then_inc(s_sel, 1)
+        S.wait_ge(s_sel, 1)
+        s_id = act(T.ident[:], T.sel[:], Exp)
+        PE.wait_ge(s_id, 1)
 
     if is_rank:
         j_me = local.index(core)
         Q.dma_start(T.xs[:], T.x[:]).then_inc(sem.loaded, 16)
         g.wait_ge(sem.loaded, 16)
-        dsts = [c for c in red if c != core]
-        eng = _deal(topo, core, dsts)
+        eng = send_deal(core)
         trs = []
-        for c in dsts:
+        for c in eng:
             k = red.index(c)
             rid, pid, _ = topo.addr(c)
             trs.append(RemoteDMATransfer(dst_ids=[DstId(rid=rid, pnc=pid)], dma_engine_mask=_mask_of(eng[c]),
@@ -114,82 +133,83 @@ def rank_program(g, core, T, topo):
         prid, ppid, _ = topo.addr(partner)
         pmask = topo.mask(core, partner)
         npe = len(_bits(pmask))
+        xp = [T.xp0, T.xp1, T.xp2, T.xp3]
+        ps = [T.ps_a, T.ps_b]
+        mtp = T.xp1[:, W:2 * W]
+        ps_t = T.xp0[:, W:2 * W]
 
-        def blk(j, a, b):
+        def blk(j):
             if local[j] == core:
-                return T.xs[:, k_me * W + a:k_me * W + b]
-            return T.land[:, j * W + a:j * W + b]
+                return T.xs[:, k_me * W:(k_me + 1) * W]
+            return T.land[:, j * W:(j + 1) * W]
 
-        n_x = sum(len(_deal(topo, c, [r for r in red if r != c])[core]) for c in local if c != core)
-        V.wait_ge(sem.xarr, n_x)
-        if is_rank:
-            V.wait_ge(sem.loaded, 16)
+        n_x = sum(len(send_deal(c)[core]) for c in local if c != core)
+        for q in (V, S):
+            q.wait_ge(sem.xarr, n_x)
+            if is_rank:
+                q.wait_ge(sem.loaded, 16)
 
-        def shift(a, b):
-            s1 = vtt(T.t1[:, a:b], blk(0, a, b), blk(1, a, b), AluOpType.max)
-            s2 = vtt(T.t2[:, a:b], blk(2, a, b), blk(3, a, b), AluOpType.max)
-            V.wait_ge(s1, 1)
-            V.wait_ge(s2, 1)
-            s3 = vtt(T.mt[:, a:b], T.t1[:, a:b], T.t2[:, a:b], AluOpType.max)
-            V.wait_ge(s3, 1)
-            return s3
-
-        def weights(j, a, b):
-            sd = vtt(T.d[:, j * W + a:j * W + b], blk(j, a, b), T.mt[:, a:b], AluOpType.subtract)
-            S.wait_ge(sd, 1)
-            sp = new_sem()
-            S.activation(T.p[:, j * W + a:j * W + b], T.d[:, j * W + a:j * W + b],
-                         ActivationFunctionType.Exp).then_inc(sp, 1)
-            return sp
-
-        H = 32
-        s_ma = shift(0, H)
-        sp = {0: [weights(0, 0, H)]}
-        s_mb = shift(H, W)
-        g.wait_ge(s_ma, 1)
-        g.wait_ge(s_mb, 1)
+        s_c = {}
+        for j in (2, 3, 0, 1):
+            s_c[j] = act(xp[j][:, 0:W], blk(j), Copy)
+        s1 = vtt(T.t1[:], blk(0), blk(1), AluOpType.max)
+        V.wait_ge(s1, 1)
+        V.wait_ge(s_c[2], 1)
+        s2 = vtt(T.t2[:], T.t1[:], xp[2][:, 0:W], AluOpType.max)
+        V.wait_ge(s2, 1)
+        V.wait_ge(s_c[3], 1)
+        s_m = vtt(T.mt[:], T.t2[:], xp[3][:, 0:W], AluOpType.max)
+        V.wait_ge(s_m, 1)
+        g.wait_ge(s_m, 1)
         g.remote_dma(T.mrem[:], T.mt[:], sem.marr, sem.sent, ppid, prid, pmask)
         sent += npe
-        sp[0].append(weights(0, H, W))
-        for j in range(1, len(local)):
-            sp[j] = [weights(j, 0, W)]
-        PE.wait_ge(s_id, 1)
-        s_sum = new_sem()
-        for j in range(len(local)):
-            for s in sp[j]:
-                PE.wait_ge(s, 1)
-            mm = PE.matmul(T.ps_s[:, 0:W], T.ident[:], T.p[:, j * W:(j + 1) * W], j == 0, j == len(local) - 1)
-        mm.then_inc(s_sum, 1)
-        V.wait_ge(s_sum, 1)
-        s_cp = new_sem()
-        V.tensor_copy(T.ssb[:], T.ps_s[:, 0:W]).then_inc(s_cp, 1)
-        g.wait_ge(s_cp, 1)
+
+        V.wait_ge(s_c[0], 1)
+        V.wait_ge(s_c[1], 1)
+        halves = [(0, W // 2), (W // 2, W)]
+        s_sum = []
+        for h, (a, b) in enumerate(halves):
+            for j in range(4):
+                lo, hi = j * W + a, j * W + b
+                sd = vtt(T.d[:, lo:hi], xp[j][:, a:b], T.mt[:, a:b], AluOpType.subtract)
+                S.wait_ge(sd, 1)
+                sp = act(T.p[:, lo:hi], T.d[:, lo:hi], Exp)
+                PE.wait_ge(sp, 1)
+                mm = PE.matmul(ps[h][:, 0:b - a], T.ident[:], T.p[:, lo:hi], j == 0, j == 3)
+            s_sum.append(new_sem())
+            mm.then_inc(s_sum[h], 1)
+        for h, (a, b) in enumerate(halves):
+            V.wait_ge(s_sum[h], 1)
+            s_cp = new_sem()
+            V.tensor_copy(T.ssb[:, a:b], ps[h][:, 0:b - a]).then_inc(s_cp, 1)
+            V.wait_ge(s_cp, 1)
+            g.wait_ge(s_cp, 1)
         g.remote_dma(T.srem[:], T.ssb[:], sem.sarr, sem.sent, ppid, prid, pmask)
         sent += npe
 
+        S.wait_ge(s_m, 1)
+        s_mp = act(mtp, T.mt[:], Copy)
+        V.wait_ge(s_mp, 1)
         V.wait_ge(sem.marr, npe)
-        s_dd = vtt(T.dd[:], T.mrem[:], T.mt[:], AluOpType.subtract)
+        s_dd = vtt(T.dd[:], T.mrem[:], mtp, AluOpType.subtract)
         V.wait_ge(s_dd, 1)
         s_cl = new_sem()
         V.tensor_scalar(T.dd[:], T.dd[:], 60.0, None, AluOpType.min).then_inc(s_cl, 1)
         S.wait_ge(s_cl, 1)
-        s_e = new_sem()
-        S.activation(T.ps_e[:, 0:W], T.dd[:], ActivationFunctionType.Exp).then_inc(s_e, 1)
-        V.wait_ge(s_cp, 1)
+        s_e = act(T.ps_e[:, 0:W], T.dd[:], Exp)
         V.wait_ge(s_e, 1)
         V.wait_ge(sem.sarr, npe)
-        s_t = vtt(T.ps_t[:, 0:W], T.srem[:], T.ps_e[:, 0:W], AluOpType.mult)
+        s_t = vtt(ps_t, T.srem[:], T.ps_e[:, 0:W], AluOpType.mult)
         V.wait_ge(s_t, 1)
-        s_den = vtt(T.den[:], T.ps_t[:, 0:W], T.ssb[:], AluOpType.add)
+        s_den = vtt(T.den[:], ps_t, T.ssb[:], AluOpType.add)
         V.wait_ge(s_den, 1)
         s_w = new_sem()
         V.reciprocal(T.ps_w[:, 0:W], T.den[:]).then_inc(s_w, 1)
         V.wait_ge(s_w, 1)
 
-        dsts = [c for c in local if c != core]
-        eng = _deal(topo, core, dsts)
+        eng = ret_deal(core)
         trs = []
-        for c in dsts:
+        for c in eng:
             j = local.index(c)
             s_y = vtt(T.ys[:, j * W:(j + 1) * W], T.p[:, j * W:(j + 1) * W], T.ps_w[:, 0:W], AluOpType.mult)
             g.wait_ge(s_y, 1)
@@ -204,7 +224,7 @@ def rank_program(g, core, T, topo):
                         AluOpType.mult)
 
     if is_rank:
-        n_y = sum(len(_deal(topo, r, [c for c in local if c != r])[core]) for r in red if r != core)
+        n_y = sum(len(ret_deal(r)[core]) for r in red if r != core)
         Q.wait_ge(sem.yarr, n_y)
         if own_y is not None:
             Q.wait_ge(own_y, 1)

@@ -2,9 +2,13 @@ from concourse.bass import DstId, RemoteDMATransfer
 from concourse.mybir import AluOpType, ActivationFunctionType
 
 W = 128
+RB = 32
 NPOOL = 48
 SCRATCH = {
-    "xs": ("sbuf", [128, 512], "float32"),
+    "xd": ("dram", [4, 128, W], "float32"),
+    "yd": ("dram", [4, 128, W], "bfloat16"),
+    "own": ("sbuf", [128, W], "float32"),
+    "yo": ("sbuf", [128, W], "bfloat16"),
     "land": ("sbuf", [128, 512], "float32"),
     "t1": ("sbuf", [128, W], "float32"),
     "t2": ("sbuf", [128, W], "float32"),
@@ -20,7 +24,6 @@ SCRATCH = {
     "dd": ("sbuf", [128, W], "float32"),
     "den": ("sbuf", [128, W], "float32"),
     "ys": ("sbuf", [128, 512], "bfloat16"),
-    "yb": ("sbuf", [128, 512], "bfloat16"),
     "xp0": ("psum", [128, 512], "float32"),
     "xp1": ("psum", [128, 512], "float32"),
     "xp2": ("psum", [128, 512], "float32"),
@@ -30,7 +33,8 @@ SCRATCH = {
     "ps_e": ("psum", [128, 512], "float32"),
     "ps_w": ("psum", [128, 512], "float32"),
 }
-SEMAPHORES = ["loaded", "stored", "xarr", "marr", "sarr", "yarr", "sent"] + ["c%d" % i for i in range(NPOOL)]
+SEMAPHORES = (["ld0", "ld1", "ldo", "stored", "xarr", "marr", "sarr", "ya0", "ya1", "ya2", "ya3", "sent"]
+              + ["c%d" % i for i in range(NPOOL)])
 
 
 def _bits(m):
@@ -44,16 +48,6 @@ def _mask_of(engines):
     return m
 
 
-def _deal(topo, core, dsts):
-    eng = _bits(topo.mask(core, dsts[0]))
-    per = 1
-    while per * 2 * len(dsts) <= len(eng):
-        per *= 2
-    pool = eng[0::2] + eng[1::2]
-    order = [c for c in dsts if topo.die(c) != topo.die(core)] + [c for c in dsts if topo.die(c) == topo.die(core)]
-    return {c: pool[i * per:(i + 1) * per] for i, c in enumerate(order)}
-
-
 def rank_program(g, core, T, topo):
     chips = sorted(set(topo.chip(c) for c in T.cores))
     here = topo.chip(core)
@@ -65,7 +59,7 @@ def rank_program(g, core, T, topo):
     def reducers(ch, other):
         far = ranks_of[other][0]
         cs = [c for c in range(topo.CORES_PER_CHIP * topo.CHIPS) if topo.chip(c) == ch and topo.may_write(c, far)]
-        return sorted(cs, key=lambda c: (topo.die(c), c))
+        return sorted(cs, key=lambda c: (c in T.cores, topo.die(c), c))
 
     red = reducers(here, there)
     red_far = reducers(there, here)
@@ -75,11 +69,19 @@ def rank_program(g, core, T, topo):
     if not (is_rank or is_red):
         return
 
-    def send_deal(c):
-        return _deal(topo, c, [r for r in red if r != c])
+    def waves_of(c):
+        waves = []
+        for part in (red[0:2], red[2:4]):
+            dsts = sorted([r for r in part if r != c], key=lambda r: topo.die(r) == topo.die(c))
+            eng = _bits(topo.mask(c, dsts[0]))
+            n = len(dsts)
+            waves.append({r: eng[i::n] for i, r in enumerate(dsts)})
+        return waves
 
-    def ret_deal(r):
-        return _deal(topo, r, [c for c in local if c != r])
+    def ret_order(r):
+        k = red.index(r)
+        n = len(local)
+        return [local[(k + t) % n] for t in range(n) if local[(k + t) % n] != r]
 
     V, S, PE, Q = g.vector, g.scalar, g.tensor, g.sync
     Exp, Copy = ActivationFunctionType.Exp, ActivationFunctionType.Copy
@@ -102,6 +104,17 @@ def rank_program(g, core, T, topo):
         return s
 
     sent = 0
+    if is_rank:
+        j_me = local.index(core)
+        waves = waves_of(core)
+        for w, wave in enumerate(waves):
+            ks = sorted(red.index(r) for r in wave)
+            lo, hi = ks[0], ks[-1] + 1
+            Q.dma_start(T.xd[lo:hi], T.x[lo * RB:hi * RB, :]).then_inc(sem["ld%d" % w], 16)
+        if is_red:
+            k = red.index(core)
+            Q.dma_start(T.own[:], T.x[k * RB:(k + 1) * RB, :]).then_inc(sem.ldo, 16)
+
     if is_red:
         s_zer, s_sel = new_sem(), new_sem()
         V.memset(T.zer[:], 0.0).then_inc(s_zer, 1)
@@ -112,19 +125,16 @@ def rank_program(g, core, T, topo):
         PE.wait_ge(s_id, 1)
 
     if is_rank:
-        j_me = local.index(core)
-        Q.dma_start(T.xs[:], T.x[:]).then_inc(sem.loaded, 16)
-        g.wait_ge(sem.loaded, 16)
-        eng = send_deal(core)
-        trs = []
-        for c in eng:
-            k = red.index(c)
-            rid, pid, _ = topo.addr(c)
-            trs.append(RemoteDMATransfer(dst_ids=[DstId(rid=rid, pnc=pid)], dma_engine_mask=_mask_of(eng[c]),
-                                         remote_sem=sem.xarr, src=T.xs[:, k * W:(k + 1) * W],
-                                         dst=T.land[:, j_me * W:(j_me + 1) * W]))
-            sent += len(eng[c])
-        g.remote_dma_fused(trs, local_sem=sem.sent)
+        for w, wave in enumerate(waves):
+            g.wait_ge(sem["ld%d" % w], 16)
+            trs = []
+            for c in wave:
+                rid, pid, _ = topo.addr(c)
+                trs.append(RemoteDMATransfer(dst_ids=[DstId(rid=rid, pnc=pid)], dma_engine_mask=_mask_of(wave[c]),
+                                             remote_sem=sem.xarr, src=T.xd[red.index(c)],
+                                             dst=T.land[:, j_me * W:(j_me + 1) * W]))
+                sent += len(wave[c])
+            g.remote_dma_fused(trs, local_sem=sem.sent)
 
     own_y = None
     if is_red:
@@ -140,14 +150,14 @@ def rank_program(g, core, T, topo):
 
         def blk(j):
             if local[j] == core:
-                return T.xs[:, k_me * W:(k_me + 1) * W]
+                return T.own[:]
             return T.land[:, j * W:(j + 1) * W]
 
-        n_x = sum(len(send_deal(c)[core]) for c in local if c != core)
+        n_x = sum(len(wave[core]) for c in local if c != core for wave in waves_of(c) if core in wave)
         for q in (V, S):
             q.wait_ge(sem.xarr, n_x)
             if is_rank:
-                q.wait_ge(sem.loaded, 16)
+                q.wait_ge(sem.ldo, 16)
 
         s_c = {}
         for j in (2, 3, 0, 1):
@@ -207,27 +217,29 @@ def rank_program(g, core, T, topo):
         V.reciprocal(T.ps_w[:, 0:W], T.den[:]).then_inc(s_w, 1)
         V.wait_ge(s_w, 1)
 
-        eng = ret_deal(core)
-        trs = []
-        for c in eng:
+        for c in ret_order(core):
             j = local.index(c)
             s_y = vtt(T.ys[:, j * W:(j + 1) * W], T.p[:, j * W:(j + 1) * W], T.ps_w[:, 0:W], AluOpType.mult)
             g.wait_ge(s_y, 1)
             rid, pid, _ = topo.addr(c)
-            trs.append(RemoteDMATransfer(dst_ids=[DstId(rid=rid, pnc=pid)], dma_engine_mask=_mask_of(eng[c]),
-                                         remote_sem=sem.yarr, src=T.ys[:, j * W:(j + 1) * W],
-                                         dst=T.yb[:, k_me * W:(k_me + 1) * W]))
-            sent += len(eng[c])
-        g.remote_dma_fused(trs, local_sem=sem.sent)
+            m = topo.mask(core, c)
+            g.remote_dma(T.yd[k_me], T.ys[:, j * W:(j + 1) * W], sem["ya%d" % k_me], sem.sent, pid, rid, m)
+            sent += len(_bits(m))
         if is_rank:
-            own_y = vtt(T.yb[:, k_me * W:(k_me + 1) * W], T.p[:, j_me * W:(j_me + 1) * W], T.ps_w[:, 0:W],
-                        AluOpType.mult)
+            own_y = vtt(T.yo[:], T.p[:, j_me * W:(j_me + 1) * W], T.ps_w[:, 0:W], AluOpType.mult)
 
     if is_rank:
-        n_y = sum(len(ret_deal(r)[core]) for r in red if r != core)
-        Q.wait_ge(sem.yarr, n_y)
+        due = sorted([r for r in red if r != core], key=lambda r: (red.index(r) // 2, ret_order(r).index(core)))
+        stores = 0
+        for i, r in enumerate(due):
+            k = red.index(r)
+            q = (Q, S)[i % 2]
+            q.wait_ge(sem["ya%d" % k], len(_bits(topo.mask(r, core))))
+            q.dma_start(T.y[k * RB:(k + 1) * RB, :], T.yd[k]).then_inc(sem.stored, 16)
+            stores += 1
         if own_y is not None:
-            Q.wait_ge(own_y, 1)
-        Q.dma_start(T.y[:], T.yb[:]).then_inc(sem.stored, 16)
-        Q.wait_ge(sem.stored, 16)
+            S.wait_ge(own_y, 1)
+            S.dma_start(T.y[k_me * RB:(k_me + 1) * RB, :], T.yo[:]).then_inc(sem.stored, 16)
+            stores += 1
+        Q.wait_ge(sem.stored, 16 * stores)
     g.wait_ge(sem.sent, sent)

from concourse.bass import DstId, RemoteDMATransfer
from concourse.mybir import AluOpType, ActivationFunctionType

W = 128
RB = 32
NPOOL = 48
SCRATCH = {
    "xd": ("dram", [4, 128, W], "float32"),
    "yd": ("dram", [4, 128, W], "bfloat16"),
    "own": ("sbuf", [128, W], "float32"),
    "yo": ("sbuf", [128, W], "bfloat16"),
    "land": ("sbuf", [128, 512], "float32"),
    "t1": ("sbuf", [128, W], "float32"),
    "t2": ("sbuf", [128, W], "float32"),
    "mt": ("sbuf", [128, W], "bfloat16"),
    "mrem": ("sbuf", [128, W], "bfloat16"),
    "ssb": ("sbuf", [128, W], "bfloat16"),
    "srem": ("sbuf", [128, W], "bfloat16"),
    "d": ("sbuf", [128, 512], "float32"),
    "p": ("sbuf", [128, 512], "bfloat16"),
    "zer": ("sbuf", [128, 128], "float32"),
    "sel": ("sbuf", [128, 128], "float32"),
    "ident": ("sbuf", [128, 128], "bfloat16"),
    "dd": ("sbuf", [128, W], "float32"),
    "den": ("sbuf", [128, W], "float32"),
    "ys": ("sbuf", [128, 512], "bfloat16"),
    "xp0": ("psum", [128, 512], "float32"),
    "xp1": ("psum", [128, 512], "float32"),
    "xp2": ("psum", [128, 512], "float32"),
    "xp3": ("psum", [128, 512], "float32"),
    "ps_a": ("psum", [128, 512], "float32"),
    "ps_b": ("psum", [128, 512], "float32"),
    "ps_e": ("psum", [128, 512], "float32"),
    "ps_w": ("psum", [128, 512], "float32"),
}
SEMAPHORES = (["ld0", "ld1", "ldo", "stored", "xarr", "marr", "sarr", "ya0", "ya1", "ya2", "ya3", "sent"]
              + ["c%d" % i for i in range(NPOOL)])


def _bits(m):
    return [i for i in range(m.bit_length()) if (m >> i) & 1]


def _mask_of(engines):
    m = 0
    for e in engines:
        m |= 1 << e
    return m


def rank_program(g, core, T, topo):
    chips = sorted(set(topo.chip(c) for c in T.cores))
    here = topo.chip(core)
    if here not in chips:
        return
    ranks_of = {ch: [c for c in T.cores if topo.chip(c) == ch] for ch in chips}
    there = [ch for ch in chips if ch != here][0]

    def reducers(ch, other):
        far = ranks_of[other][0]
        cs = [c for c in range(topo.CORES_PER_CHIP * topo.CHIPS) if topo.chip(c) == ch and topo.may_write(c, far)]
        return sorted(cs, key=lambda c: (c in T.cores, topo.die(c), c))

    red = reducers(here, there)
    red_far = reducers(there, here)
    local = ranks_of[here]
    is_rank = core in local
    is_red = core in red
    if not (is_rank or is_red):
        return

    def waves_of(c):
        waves = []
        for part in (red[0:2], red[2:4]):
            dsts = sorted([r for r in part if r != c], key=lambda r: topo.die(r) == topo.die(c))
            eng = _bits(topo.mask(c, dsts[0]))
            n = len(dsts)
            waves.append({r: eng[i::n] for i, r in enumerate(dsts)})
        return waves

    def ret_order(r):
        k = red.index(r)
        n = len(local)
        return [local[(k + t) % n] for t in range(n) if local[(k + t) % n] != r]

    V, S, PE, Q = g.vector, g.scalar, g.tensor, g.sync
    Exp, Copy = ActivationFunctionType.Exp, ActivationFunctionType.Copy
    sem = T.sem
    used = [0]

    def new_sem():
        s = sem["c%d" % used[0]]
        used[0] += 1
        return s

    def vtt(out, a, b, op):
        s = new_sem()
        V.tensor_tensor(out, a, b, op).then_inc(s, 1)
        return s

    def act(out, in_, func):
        s = new_sem()
        S.activation(out, in_, func).then_inc(s, 1)
        return s

    sent = 0
    if is_rank:
        j_me = local.index(core)
        waves = waves_of(core)
        for w, wave in enumerate(waves):
            ks = sorted(red.index(r) for r in wave)
            lo, hi = ks[0], ks[-1] + 1
            Q.dma_start(T.xd[lo:hi], T.x[lo * RB:hi * RB, :]).then_inc(sem["ld%d" % w], 16)
        if is_red:
            k = red.index(core)
            Q.dma_start(T.own[:], T.x[k * RB:(k + 1) * RB, :]).then_inc(sem.ldo, 16)

    if is_red:
        s_zer, s_sel = new_sem(), new_sem()
        V.memset(T.zer[:], 0.0).then_inc(s_zer, 1)
        g.wait_ge(s_zer, 1)
        g.affine_select(T.sel[:], T.zer[:], [[-1, 128]], AluOpType.is_equal, -200.0, 0, 1).then_inc(s_sel, 1)
        S.wait_ge(s_sel, 1)
        s_id = act(T.ident[:], T.sel[:], Exp)
        PE.wait_ge(s_id, 1)

    if is_rank:
        for w, wave in enumerate(waves):
            g.wait_ge(sem["ld%d" % w], 16)
            trs = []
            for c in wave:
                rid, pid, _ = topo.addr(c)
                trs.append(RemoteDMATransfer(dst_ids=[DstId(rid=rid, pnc=pid)], dma_engine_mask=_mask_of(wave[c]),
                                             remote_sem=sem.xarr, src=T.xd[red.index(c)],
                                             dst=T.land[:, j_me * W:(j_me + 1) * W]))
                sent += len(wave[c])
            g.remote_dma_fused(trs, local_sem=sem.sent)

    own_y = None
    if is_red:
        k_me = red.index(core)
        partner = red_far[k_me]
        prid, ppid, _ = topo.addr(partner)
        pmask = topo.mask(core, partner)
        npe = len(_bits(pmask))
        xp = [T.xp0, T.xp1, T.xp2, T.xp3]
        ps = [T.ps_a, T.ps_b]
        mtp = T.xp1[:, W:2 * W]
        ps_t = T.xp0[:, W:2 * W]

        def blk(j):
            if local[j] == core:
                return T.own[:]
            return T.land[:, j * W:(j + 1) * W]

        n_x = sum(len(wave[core]) for c in local if c != core for wave in waves_of(c) if core in wave)
        for q in (V, S):
            q.wait_ge(sem.xarr, n_x)
            if is_rank:
                q.wait_ge(sem.ldo, 16)

        s_c = {}
        for j in (2, 3, 0, 1):
            s_c[j] = act(xp[j][:, 0:W], blk(j), Copy)
        s1 = vtt(T.t1[:], blk(0), blk(1), AluOpType.max)
        V.wait_ge(s1, 1)
        V.wait_ge(s_c[2], 1)
        s2 = vtt(T.t2[:], T.t1[:], xp[2][:, 0:W], AluOpType.max)
        V.wait_ge(s2, 1)
        V.wait_ge(s_c[3], 1)
        s_m = vtt(T.mt[:], T.t2[:], xp[3][:, 0:W], AluOpType.max)
        V.wait_ge(s_m, 1)
        g.wait_ge(s_m, 1)
        g.remote_dma(T.mrem[:], T.mt[:], sem.marr, sem.sent, ppid, prid, pmask)
        sent += npe

        V.wait_ge(s_c[0], 1)
        V.wait_ge(s_c[1], 1)
        halves = [(0, W // 2), (W // 2, W)]
        s_sum = []
        for h, (a, b) in enumerate(halves):
            for j in range(4):
                lo, hi = j * W + a, j * W + b
                sd = vtt(T.d[:, lo:hi], xp[j][:, a:b], T.mt[:, a:b], AluOpType.subtract)
                S.wait_ge(sd, 1)
                sp = act(T.p[:, lo:hi], T.d[:, lo:hi], Exp)
                PE.wait_ge(sp, 1)
                mm = PE.matmul(ps[h][:, 0:b - a], T.ident[:], T.p[:, lo:hi], j == 0, j == 3)
            s_sum.append(new_sem())
            mm.then_inc(s_sum[h], 1)
        for h, (a, b) in enumerate(halves):
            V.wait_ge(s_sum[h], 1)
            s_cp = new_sem()
            V.tensor_copy(T.ssb[:, a:b], ps[h][:, 0:b - a]).then_inc(s_cp, 1)
            V.wait_ge(s_cp, 1)
            g.wait_ge(s_cp, 1)
        g.remote_dma(T.srem[:], T.ssb[:], sem.sarr, sem.sent, ppid, prid, pmask)
        sent += npe

        S.wait_ge(s_m, 1)
        s_mp = act(mtp, T.mt[:], Copy)
        V.wait_ge(s_mp, 1)
        V.wait_ge(sem.marr, npe)
        s_dd = vtt(T.dd[:], T.mrem[:], mtp, AluOpType.subtract)
        V.wait_ge(s_dd, 1)
        s_cl = new_sem()
        V.tensor_scalar(T.dd[:], T.dd[:], 60.0, None, AluOpType.min).then_inc(s_cl, 1)
        S.wait_ge(s_cl, 1)
        s_e = act(T.ps_e[:, 0:W], T.dd[:], Exp)
        V.wait_ge(s_e, 1)
        V.wait_ge(sem.sarr, npe)
        s_t = vtt(ps_t, T.srem[:], T.ps_e[:, 0:W], AluOpType.mult)
        V.wait_ge(s_t, 1)
        s_den = vtt(T.den[:], ps_t, T.ssb[:], AluOpType.add)
        V.wait_ge(s_den, 1)
        s_w = new_sem()
        V.reciprocal(T.ps_w[:, 0:W], T.den[:]).then_inc(s_w, 1)
        V.wait_ge(s_w, 1)

        for c in ret_order(core):
            j = local.index(c)
            s_y = vtt(T.ys[:, j * W:(j + 1) * W], T.p[:, j * W:(j + 1) * W], T.ps_w[:, 0:W], AluOpType.mult)
            g.wait_ge(s_y, 1)
            rid, pid, _ = topo.addr(c)
            m = topo.mask(core, c)
            g.remote_dma(T.yd[k_me], T.ys[:, j * W:(j + 1) * W], sem["ya%d" % k_me], sem.sent, pid, rid, m)
            sent += len(_bits(m))
        if is_rank:
            own_y = vtt(T.yo[:], T.p[:, j_me * W:(j_me + 1) * W], T.ps_w[:, 0:W], AluOpType.mult)

    if is_rank:
        due = sorted([r for r in red if r != core], key=lambda r: (red.index(r) // 2, ret_order(r).index(core)))
        stores = 0
        for i, r in enumerate(due):
            k = red.index(r)
            q = (Q, S)[i % 2]
            q.wait_ge(sem["ya%d" % k], len(_bits(topo.mask(r, core))))
            q.dma_start(T.y[k * RB:(k + 1) * RB, :], T.yd[k]).then_inc(sem.stored, 16)
            stores += 1
        if own_y is not None:
            S.wait_ge(own_y, 1)
            S.dma_start(T.y[k_me * RB:(k_me + 1) * RB, :], T.yo[:]).then_inc(sem.stored, 16)
            stores += 1
        Q.wait_ge(sem.stored, 16 * stores)
    g.wait_ge(sem.sent, sent)
